import numpy as np
import ml_dtypes


def mxq(x, axis, fmt="e4m3"):
    dtype, down = {"e4m3": (ml_dtypes.float8_e4m3fn, 7), "e5m2": (ml_dtypes.float8_e5m2, 14)}[fmt]
    v = np.moveaxis(np.asarray(x, np.float32).astype(ml_dtypes.bfloat16).astype(np.float64), axis, -1)
    blocks = v.reshape(v.shape[:-1] + (-1, 32))
    amax = np.abs(blocks).max(-1, keepdims=True)
    byte = np.maximum(np.where(amax > 0, np.frexp(amax)[1] - 1 + 127, 0) - down, 1)
    scale = np.exp2(byte - 127.0)
    codes = (blocks / scale).astype(np.float32).astype(dtype).astype(np.float64)
    return np.moveaxis((codes * scale).reshape(v.shape), -1, axis)


WIDE = False


def mx_kscale(k):
    if not WIDE:
        return np.ones(k)
    levels = np.array([10, -10, 5, -5, 0])
    if k % 512:
        return np.exp2(np.random.permutation(np.resize(levels, k // 32))).repeat(32)
    a = np.empty((k // 512, 16))
    for p in range(k // 512):
        a[p, :8] = np.random.permutation(np.resize(levels, 8))
        for g in range(8):
            far = levels[np.abs(levels - a[p, g]) >= 10]
            a[p, g + 8] = far[np.random.randint(len(far))]
    return np.exp2(a.ravel()).repeat(32)


BF16 = ml_dtypes.bfloat16


def bf(x):
    return np.asarray(x, np.float32).astype(BF16)


def f64(x):
    return np.asarray(x).astype(np.float64)

def planes(Y):
    n, m = Y.shape
    b = f64(bf(Y)).reshape(n // 32, 32, m)
    amax = np.abs(b).max(1)
    byte = np.clip(np.where(amax > 0, np.frexp(amax)[1] - 1 + 127 - 7, 1), 1, 254)
    codes = (b * np.exp2(127.0 - byte)[:, None, :]).reshape(n, m).astype(np.float32).astype(ml_dtypes.float8_e4m3fn).view(np.uint8)
    words = codes.reshape(n // 512, 128, 4, m).transpose(0, 1, 3, 2)
    return np.ascontiguousarray(words), np.ascontiguousarray(byte.astype(np.uint8).reshape(n // 512, 16, m))


N, D, R, C, K = 1024, 1024, 512, 512, 2


def setup_inputs():
    s = mx_kscale(D)
    t = np.stack([mx_kscale(R) for _ in range(K)])
    return {
        "x": bf(np.random.standard_normal((N, D)) * s),
        "w1": bf(np.random.standard_normal((D, C)) / np.sqrt(D) / s[:, None]),
        "u": bf(np.random.standard_normal((K, D, R)) / np.sqrt(D) / s[None, :, None]),
        "lam": bf(np.random.standard_normal((K, R)) * 0.5 * t),
        "w": bf(np.random.standard_normal((K, R, C)) / np.sqrt(R) / t[:, :, None]),
        "b": bf(np.random.standard_normal(C) * 0.3),
    }


def core(x, w1, u, lam, w, b):
    u, lam, w = f64(u), f64(lam), f64(w)
    xq = mxq(f64(x), 1, "e4m3")
    q2 = xq @ mxq(u[0], 0, "e4m3")
    q3 = xq @ mxq(u[1], 0, "e4m3")
    p2 = lam[0][None, :] * q2 * q2
    p3 = lam[1][None, :] * q3 * q3 * q3
    y1 = xq @ mxq(f64(w1), 0, "e4m3")
    y2 = mxq(p2, 1, "e4m3") @ mxq(w[0], 0, "e4m3")
    y3 = mxq(p3, 1, "e4m3") @ mxq(w[1], 0, "e4m3")
    return y1 + y2 + y3 + f64(b)[None, :]


def reference(x, w1, u, lam, w, b):
    R_out = core(x, w1, u, lam, w, b)
    words, scales = planes(R_out.T)
    return R_out, words, scales

@@ -1,0 +1,230 @@
+from contextlib import ExitStack
+
+import concourse.mybir as mybir
+from concourse.masks import make_identity
+
+N, D, R, C = 1024, 1024, 512, 512
+FLOPS = 2 * N * D * (2 * R + C) + 2 * 2 * N * R * C
+
+F32 = mybir.dt.float32
+BF16 = mybir.dt.bfloat16
+U32 = mybir.dt.uint32
+I32 = mybir.dt.int32
+U8 = mybir.dt.uint8
+FP8X4 = mybir.dt.float8_e4m3fn_x4
+MULT = mybir.AluOpType.mult
+ADD = mybir.AluOpType.add
+SQUARE = mybir.ActivationFunctionType.Square
+
+P = 128
+ORDER = (
+    "Lx0 Lx1 T0 Lu1b Lu1a Lx2 Iu1b1.V Iu1b0.V Iu1a1.V Qu1b T1 T2 CX0.A CX1.A QX00 QX01 Lu0a Iu0a1.V Iu1a0.A "
+    "Qu1a Lx3 Iu0a0.A Qu0a Lu0b Iu0b0.V CX2.A T3 CX3.A QX10 QX11 Lw1a Iw1a1.V Iu0b1.A Qu0b M300 S300 M301 M310 "
+    "S301 Lv3 Iv30.V Llam Iv31.A Lx4 Lx5 T4 T5 S310 CX4.A CX5.A M20 S20 M21 M22 P300 P301 Qv3 Iw1a0.V P310 "
+    "I30.V Lw1b Lx6 M311 T6 S21 S22 Iw1b0.A S311 CX6.A Lx7 T7 CX7.A QX20 QX21 P20 P21 P22 M23 M24 Iw1b1.V QP30 "
+    "P311 Qw1b M320 M321 QP20 QX30 QX31 S320 S23 P23 Qw1a I31.V Lv2 Iv20.A QP21 Iv21.A Qv2 P320 S24 QP31 S321 "
+    "P321 M25 S25 M26 M330 M331 M27 S330 P24 P330 P25 S331 P331 QP22 I32.A QP32 S26 S27 P26 P27 I33.A MY0 MY1 "
+    "MY2 MY3 Lb A0 SY0 QP33 QP23 A1 SY1 A2 A3 MY4 A4 MY5 MY6 MY7 C0.A C1.A TY0 TY1 C2.A TY2 C3.A C4.A A5 A6 A7 "
+    "SY2 SY3 SY4 SY5 SY6 SY7 C5.A C6.V C7.V TY3 TY4 TY5 TY6 TY7 CY0.A CY1.A CY2.A CY3.A CY4.V CY5.A QY0 QY1 SC0 "
+    "CY6.A CY7.A QY2 QY3 SC1 SC2 SC3"
+).split(" ")
+
+
+def tile_spamlowrankpolynomialorders_x1_kernel(tc, x, w1, u, lam, w, b, out_0, out_1, out_2):
+    nc = tc.nc
+    with ExitStack() as ctx:
+        keep = ctx.enter_context(tc.tile_pool(name="keep", bufs=1))
+        rot = ctx.enter_context(tc.tile_pool(name="rot", bufs=8))
+        psum = ctx.enter_context(tc.psum_pool(name="psum", bufs=1))
+        ctx.enter_context(tc.manual_schedule())
+
+        def kept(name, shape, dtype):
+            return keep.tile(shape, dtype, name=name, align_bytes=256)
+
+        weights = {
+            "u0a": u[0, 0:512, :], "u0b": u[0, 512:1024, :], "u1a": u[1, 0:512, :], "u1b": u[1, 512:1024, :],
+            "w1a": w1[0:512, :], "w1b": w1[512:1024, :], "v2": w[0], "v3": w[1],
+        }
+        raw = {k: kept("raw_" + k, [P, 4, 512], BF16) for k in weights}
+        codes = {k: kept("codes_" + k, [P, 512], U32) for k in weights}
+        scales = {k: kept("scales_" + k, [P, 512], U8) for k in weights}
+        grouped = {}
+        x_rows = [kept("x_rows%d" % t, [P, D], BF16) for t in range(8)]
+        x_grouped = kept("x_grouped", [P, 2, 4 * N], BF16)
+        x_codes = kept("x_codes", [P, 2, N], U32)
+        x_scales = kept("x_scales", [P, 2, N], U8)
+        p2 = kept("p2", [P, 4 * N], BF16)
+        p3_rows = kept("p3_rows", [P, 4, 4, 256], BF16)
+        p3 = kept("p3", [P, 4 * N], BF16)
+        p_codes = kept("p_codes", [P, 2, N], U32)
+        p_scales = kept("p_scales", [P, 2, N], U8)
+        y = [kept("y%d" % t, [P, C], F32) for t in range(8)]
+        y_bf = [kept("y_bf%d" % t, [P, C], BF16) for t in range(8)]
+        y_grouped = kept("y_grouped", [P, 4 * N], BF16)
+        y_codes = kept("y_codes", [P, N], U32)
+        y_scales = kept("y_scales", [P, N], U8)
+        ident = kept("ident", [P, P], F32)
+        lam_sb = kept("lam_sb", [P, 2, 4], BF16)
+        bias = kept("bias", [P, C], BF16)
+        warm_in = kept("warm_in", [P, 1], F32)
+        warm_out = kept("warm_out", [P, 1], F32)
+        banks = {}
+        squares = {}
+        out_words = out_1[0].rearrange("p m t -> p (m t)").bitcast(I32)
+        out_scales = out_2[0].bitcast(I32)
+
+        def new_bank(key):
+            i = len(banks) % 8
+            banks[key] = psum.tile([P, 512], F32, name="bank%d" % i, tag="bank%d" % i)
+            return banks[key]
+
+        def copy(engine, out, in_):
+            if engine == "A":
+                nc.scalar.copy(out=out, in_=in_)
+            elif engine == "V":
+                nc.vector.tensor_copy(out=out, in_=in_)
+            else:
+                nc.gpsimd.tensor_scalar(out=out, in0=in_, scalar1=1.0, scalar2=0.0, op0=MULT, op1=ADD)
+
+        def quantize(cds, scl, in_):
+            nc.vector.quantize_mx(out=cds.bitcast(FP8X4), scales=scl, in_=in_)
+
+        def mx(out, lc, ls, rc, rs, start, stop):
+            nc.tensor.matmul_mx(out=out, lhsT=lc.bitcast(FP8X4), lhsT_scale=ls, rhs=rc.bitcast(FP8X4),
+                                rhs_scale=rs, start=start, stop=stop)
+
+        def q_group(out, name, t, cols):
+            m = slice(128 * t, 128 * t + 128)
+            for g in range(2):
+                k = name + "ab"[g]
+                mx(out, codes[k][:, m], scales[k][:, m], x_codes[:, g, cols], x_scales[:, g, cols], g == 0, g == 1)
+
+        def step(name, engine):
+            if name == "Llam":
+                nc.sync.dma_start(out=lam_sb[:], in_=lam.rearrange("o (p j) -> p o j", j=4))
+            elif name == "Lb":
+                nc.sync.dma_start(out=bias[:], in_=b.partition_broadcast(P))
+            elif name[0] == "L" and name[1] == "x":
+                t = int(name[2])
+                nc.sync.dma_start(out=x_rows[t][:], in_=x[128 * t : 128 * t + 128, :])
+            elif name[0] == "L":
+                k = name[1:]
+                nc.sync.dma_start(out=raw[k][:], in_=weights[k].rearrange("(p j) c -> p j c", j=4))
+            elif name[:2] == "I3":
+                q = int(name[2])
+                dst = p3[:, 1024 * q : 1024 * q + 1024].rearrange("p (c i j) -> p c j i", i=4, j=4)
+                copy(engine, dst, p3_rows[:, q, :, :].rearrange("p j (c i) -> p c j i", i=4))
+            elif name[0] == "I":
+                k, h = name[1:-1], int(name[-1])
+                if k not in grouped:
+                    grouped[k] = rot.tile([P, 2048], BF16, name="grouped", tag="grouped", align_bytes=256)
+                if k[0] == "u":
+                    dst = grouped[k][:].rearrange("p (t a i j) -> p a t i j", t=4, i=2, j=4)
+                    src = raw[k][:].rearrange("p j (a i t) -> p a t i j", i=2, t=4)
+                    copy(engine, dst[:, 32 * h : 32 * h + 32], src[:, 32 * h : 32 * h + 32])
+                else:
+                    dst = grouped[k][:].rearrange("p (c i j) -> p c j i", i=4, j=4)
+                    src = raw[k][:].rearrange("p j (c i) -> p c j i", i=4)
+                    copy(engine, dst[:, 64 * h : 64 * h + 64], src[:, 64 * h : 64 * h + 64])
+            elif name[:2] == "QX":
+                q, g = int(name[2]), int(name[3])
+                cols = slice(256 * q, 256 * q + 256)
+                quantize(x_codes[:, g, cols], x_scales[:, g, cols], x_grouped[:, g, 1024 * q : 1024 * q + 1024])
+            elif name[:2] == "QP":
+                o, q = int(name[2]) - 2, int(name[3])
+                cols = slice(256 * q, 256 * q + 256)
+                quantize(p_codes[:, o, cols], p_scales[:, o, cols], (p2, p3)[o][:, 1024 * q : 1024 * q + 1024])
+            elif name[:2] == "QY":
+                q = int(name[2])
+                cols = slice(256 * q, 256 * q + 256)
+                quantize(y_codes[:, cols], y_scales[:, cols], y_grouped[:, 1024 * q : 1024 * q + 1024])
+            elif name[0] == "Q":
+                k = name[1:]
+                quantize(codes[k][:], scales[k][:], grouped[k][:])
+            elif name[:2] == "TY":
+                t = int(name[2])
+                bank = new_bank(name)
+                words = y_bf[t][:].bitcast(F32)
+                for h in range(2):
+                    nc.tensor.transpose(bank[:, 128 * h : 128 * h + 128], words[:, h:256:2], ident[:])
+            elif name[0] == "T":
+                t = int(name[1])
+                bank = new_bank(name)
+                words = x_rows[t][:].bitcast(F32)
+                for g in range(2):
+                    for h in range(2):
+                        c0 = 128 * (2 * g + h)
+                        nc.tensor.transpose(bank[:, c0 : c0 + 128], words[:, 256 * g + h : 256 * g + 256 : 2], ident[:])
+            elif name[:2] == "CX":
+                t = int(name[2])
+                dst = x_grouped[:].bitcast(F32)[:, :, 256 * t : 256 * t + 256].rearrange("p g (n h) -> p g n h", h=2)
+                copy(engine, dst, banks["T%d" % t][:].rearrange("p (g h n) -> p g n h", g=2, h=2))
+            elif name[:2] == "CY":
+                t = int(name[2])
+                dst = y_grouped[:].bitcast(F32)[:, 256 * t : 256 * t + 256].rearrange("p (n h) -> p n h", h=2)
+                copy(engine, dst, banks["TY%d" % t][:, 0:256].rearrange("p (h n) -> p n h", h=2))
+            elif name[0] == "C":
+                t = int(name[1])
+                copy(engine, y_bf[t][:], y[t][:])
+            elif name[:2] == "M2":
+                t = int(name[2])
+                bank = new_bank(name)
+                for j in range(4):
+                    q_group(bank[:, 128 * j : 128 * j + 128], "u0", j, slice(128 * t, 128 * t + 128))
+            elif name[:2] == "M3":
+                q, h = int(name[2]), int(name[3])
+                bank = new_bank(name)
+                for j in range(2):
+                    q_group(bank[:, 256 * j : 256 * j + 256], "u1", 2 * h + j, slice(256 * q, 256 * q + 256))
+            elif name[:2] == "S2":
+                squares[name] = rot.tile([P, 512], F32, name="square", tag="square")
+                nc.scalar.activation(out=squares[name][:].rearrange("p (n j) -> p n j", j=4),
+                                     in_=banks["M2" + name[2:]][:].rearrange("p (j n) -> p n j", j=4), func=SQUARE)
+            elif name[:2] == "S3":
+                squares[name] = rot.tile([P, 512], F32, name="square", tag="square")
+                nc.scalar.activation(out=squares[name][:], in_=banks["M3" + name[2:]][:], func=SQUARE)
+            elif name[:2] == "P2":
+                t = int(name[2])
+                nc.vector.tensor_tensor(
+                    out=p2[:, 512 * t : 512 * t + 512].rearrange("p (n j) -> p n j", j=4),
+                    in0=squares["S2%d" % t][:].rearrange("p (n j) -> p n j", j=4),
+                    in1=lam_sb[:, 0, :].unsqueeze(1).to_broadcast([P, 128, 4]), op=MULT)
+            elif name[:2] == "P3":
+                q, h = int(name[2]), int(name[3])
+                for j in range(2):
+                    cols = slice(256 * j, 256 * j + 256)
+                    t = 2 * h + j
+                    nc.vector.scalar_tensor_tensor(
+                        out=p3_rows[:, q, t, :], in0=squares["S3" + name[2:]][:, cols], scalar=lam_sb[:, 1, t : t + 1],
+                        in1=banks["M3" + name[2:]][:, cols], op0=MULT, op1=MULT)
+            elif name[:2] == "MY":
+                t = int(name[2])
+                bank = new_bank(name)
+                m = slice(128 * t, 128 * t + 128)
+                for g in range(2):
+                    k = "w1" + "ab"[g]
+                    mx(bank[:], x_codes[:, g, m], x_scales[:, g, m], codes[k][:], scales[k][:], g == 0, False)
+                for o in range(2):
+                    k = "v%d" % (o + 2)
+                    mx(bank[:], p_codes[:, o, m], p_scales[:, o, m], codes[k][:], scales[k][:], False, o == 1)
+            elif name[0] == "A":
+                t = int(name[1])
+                nc.vector.tensor_tensor(out=y[t][:], in0=banks["MY%d" % t][:], in1=bias[:], op=ADD)
+            elif name[:2] == "SY":
+                t = int(name[2])
+                nc.sync.dma_start(out=out_0[128 * t : 128 * t + 128, :], in_=y[t][:])
+            else:
+                q = int(name[2])
+                cols = slice(256 * q, 256 * q + 256)
+                nc.sync.dma_start(out=out_words[:, cols], in_=y_codes[:, cols].bitcast(I32))
+
+        nc.gpsimd.memset(warm_in[:], 0.0)
+        nc.scalar.activation(out=warm_out[:], in_=warm_in[:], func=SQUARE)
+        make_identity(nc, ident[:])
+        for s in ORDER:
+            parts = s.split(".")
+            step(parts[0], parts[-1])
+        for quad in range(4):
+            queue = (nc.sync, nc.scalar)[quad % 2]
+            queue.dma_start(out=out_scales[4 * quad : 4 * quad + 4, :],
+                            in_=y_scales[32 * quad : 32 * quad + 4, :].bitcast(I32))

@@ -18,15 +18,15 @@ SQUARE = mybir.ActivationFunctionType.Square
 
 P = 128
 ORDER = (
-    "Lx0 Lx1 T0 Lu1b Lu1a Lx2 Iu1b1.V Iu1b0.V Iu1a1.V Qu1b T1 T2 CX0.A CX1.A QX00 QX01 Lu0a Iu0a1.V Iu1a0.A "
-    "Qu1a Lx3 Iu0a0.A Qu0a Lu0b Iu0b0.V CX2.A T3 CX3.A QX10 QX11 Lw1a Iw1a1.V Iu0b1.A Qu0b M300 S300 M301 M310 "
-    "S301 Lv3 Iv30.V Llam Iv31.A Lx4 Lx5 T4 T5 S310 CX4.A CX5.A M20 S20 M21 M22 P300 P301 Qv3 Iw1a0.V P310 "
-    "I30.V Lw1b Lx6 M311 T6 S21 S22 Iw1b0.A S311 CX6.A Lx7 T7 CX7.A QX20 QX21 P20 P21 P22 M23 M24 Iw1b1.V QP30 "
-    "P311 Qw1b M320 M321 QP20 QX30 QX31 S320 S23 P23 Qw1a I31.V Lv2 Iv20.A QP21 Iv21.A Qv2 P320 S24 QP31 S321 "
-    "P321 M25 S25 M26 M330 M331 M27 S330 P24 P330 P25 S331 P331 QP22 I32.A QP32 S26 S27 P26 P27 I33.A MY0 MY1 "
-    "MY2 MY3 Lb A0 SY0 QP33 QP23 A1 SY1 A2 A3 MY4 A4 MY5 MY6 MY7 C0.A C1.A TY0 TY1 C2.A TY2 C3.A C4.A A5 A6 A7 "
-    "SY2 SY3 SY4 SY5 SY6 SY7 C5.A C6.V C7.V TY3 TY4 TY5 TY6 TY7 CY0.A CY1.A CY2.A CY3.A CY4.V CY5.A QY0 QY1 SC0 "
-    "CY6.A CY7.A QY2 QY3 SC1 SC2 SC3"
+    "Lu1b Iu1b0.V Iu1b1.V Qu1b Lx0 Lx1 Lu1a Iu1a1.V Lu0a Iu0a1.V Iu1a0.A Qu1a T00 T01 CX00.A QX00 CX01.A QX01 "
+    "M300 Lu0b Iu0b0.V Lv2 Iv21.V Iu0a0.A Qu0a Lw1b Iw1b1.V Iw1b0.V Iv20.A Qv2 Iu0b1.A Qu0b Qw1b Lx2 Lx3 Lx4 "
+    "Lx5 Lx6 S300 M301 S301 T10 T11 CX10.A QX10 CX11.A T20 T21 CX20.A Llam P300 QX11 CX21.A M20 S20 Lx7 T30 "
+    "CX30.A QX20 P301 I30.A Lv3 Iv30.V QX21 P20 Lw1a Iw1a0.V Iw1a1.V M310 S310 P310 QX30 T31 M311 S311 CX31.A "
+    "P311 M21 S21 P21 M22 S22 QP30 QX31 Iv31.A QP20 Qw1a P22 Qv3 M23 S23 P23 M320 S320 P320 M24 M25 S24 QP21 "
+    "M321 M330 S321 P321 P24 I31.A QP31 S25 P25 M26 M331 MY0 Lb A0 QP22 I32.A QP32 S330 S331 P330 P331 S26 M27 "
+    "S27 P26 P27 MY1 SY0 A1 SY1 MY2 MY3 MY4 QP23 I33.A QP33 A2 SY2 A3 A4 MY5 A5 MY6 MY7 A6 SY3 SY4 SY5 A7 SY6 "
+    "SY7 C0.A TY0 C1.A TY1 C2.A C3.A C4.A C5.A C6.V C7.V TY2 TY3 TY4 CY0.A CY1.A CY2.A CY3.V QY0 QY1 TY5 TY6 "
+    "CY4.A CY5.A CY6.A TY7 CY7.V QY2 QY3 SC0 SC1 SC2 SC3"
 ).split(" ")
 
 
@@ -121,7 +121,7 @@ def tile_spamlowrankpolynomialorders_x1_kernel(tc, x, w1, u, lam, w, b, out_0, o
                 if k[0] == "u":
                     dst = grouped[k][:].rearrange("p (t a i j) -> p a t i j", t=4, i=2, j=4)
                     src = raw[k][:].rearrange("p j (a i t) -> p a t i j", i=2, t=4)
-                    copy(engine, dst[:, 32 * h : 32 * h + 32], src[:, 32 * h : 32 * h + 32])
+                    copy(engine, dst[:, :, 2 * h : 2 * h + 2], src[:, :, 2 * h : 2 * h + 2])
                 else:
                     dst = grouped[k][:].rearrange("p (c i j) -> p c j i", i=4, j=4)
                     src = raw[k][:].rearrange("p j (c i) -> p c j i", i=4)
@@ -139,8 +139,13 @@ def tile_spamlowrankpolynomialorders_x1_kernel(tc, x, w1, u, lam, w, b, out_0, o
                 cols = slice(256 * q, 256 * q + 256)
                 quantize(y_codes[:, cols], y_scales[:, cols], y_grouped[:, 1024 * q : 1024 * q + 1024])
             elif name[0] == "Q":
-                k = name[1:]
-                quantize(codes[k][:], scales[k][:], grouped[k][:])
+                if name[1:] in weights:
+                    k = name[1:]
+                    quantize(codes[k][:], scales[k][:], grouped[k][:])
+                else:
+                    k, h = name[1:-1], int(name[-1])
+                    cols = slice(256 * h, 256 * h + 256)
+                    quantize(codes[k][:, cols], scales[k][:, cols], grouped[k][:, 1024 * h : 1024 * h + 1024])
             elif name[:2] == "TY":
                 t = int(name[2])
                 bank = new_bank(name)
@@ -148,17 +153,17 @@ def tile_spamlowrankpolynomialorders_x1_kernel(tc, x, w1, u, lam, w, b, out_0, o
                 for h in range(2):
                     nc.tensor.transpose(bank[:, 128 * h : 128 * h + 128], words[:, h:256:2], ident[:])
             elif name[0] == "T":
-                t = int(name[1])
+                q, g = int(name[1]), int(name[2])
                 bank = new_bank(name)
-                words = x_rows[t][:].bitcast(F32)
-                for g in range(2):
+                for a in range(2):
+                    words = x_rows[2 * q + a][:].bitcast(F32)
                     for h in range(2):
-                        c0 = 128 * (2 * g + h)
+                        c0 = 128 * (2 * a + h)
                         nc.tensor.transpose(bank[:, c0 : c0 + 128], words[:, 256 * g + h : 256 * g + 256 : 2], ident[:])
             elif name[:2] == "CX":
-                t = int(name[2])
-                dst = x_grouped[:].bitcast(F32)[:, :, 256 * t : 256 * t + 256].rearrange("p g (n h) -> p g n h", h=2)
-                copy(engine, dst, banks["T%d" % t][:].rearrange("p (g h n) -> p g n h", g=2, h=2))
+                q, g = int(name[2]), int(name[3])
+                dst = x_grouped[:, g, 1024 * q : 1024 * q + 1024].bitcast(F32).rearrange("p (a n h) -> p a n h", a=2, h=2)
+                copy(engine, dst, banks["T" + name[2:]][:].rearrange("p (a h n) -> p a n h", a=2, h=2))
             elif name[:2] == "CY":
                 t = int(name[2])
                 dst = y_grouped[:].bitcast(F32)[:, 256 * t : 256 * t + 256].rearrange("p (n h) -> p n h", h=2)

@@ -18,16 +18,16 @@ SQUARE = mybir.ActivationFunctionType.Square
 
 P = 128
 ORDER = (
-    "Lu1b Iu1b0.V Iu1b1.V Qu1b Lx0 Lx1 Lu1a Iu1a1.V Lu0a Iu0a1.V Iu1a0.A Qu1a T00 T01 CX00.A QX00 CX01.A QX01 "
-    "M300 Lu0b Iu0b0.V Lv2 Iv21.V Iu0a0.A Qu0a Lw1b Iw1b1.V Iw1b0.V Iv20.A Qv2 Iu0b1.A Qu0b Qw1b Lx2 Lx3 Lx4 "
-    "Lx5 Lx6 S300 M301 S301 T10 T11 CX10.A QX10 CX11.A T20 T21 CX20.A Llam P300 QX11 CX21.A M20 S20 Lx7 T30 "
-    "CX30.A QX20 P301 I30.A Lv3 Iv30.V QX21 P20 Lw1a Iw1a0.V Iw1a1.V M310 S310 P310 QX30 T31 M311 S311 CX31.A "
-    "P311 M21 S21 P21 M22 S22 QP30 QX31 Iv31.A QP20 Qw1a P22 Qv3 M23 S23 P23 M320 S320 P320 M24 M25 S24 QP21 "
-    "M321 M330 S321 P321 P24 I31.A QP31 S25 P25 M26 M331 MY0 Lb A0 QP22 I32.A QP32 S330 S331 P330 P331 S26 M27 "
-    "S27 P26 P27 MY1 SY0 A1 SY1 MY2 MY3 MY4 QP23 I33.A QP33 A2 SY2 A3 A4 MY5 A5 MY6 MY7 A6 SY3 SY4 SY5 A7 SY6 "
-    "SY7 C0.A TY0 C1.A TY1 C2.A C3.A C4.A C5.A C6.V C7.V TY2 TY3 TY4 CY0.A CY1.A CY2.A CY3.V QY0 QY1 TY5 TY6 "
-    "CY4.A CY5.A CY6.A TY7 CY7.V QY2 QY3 SC0 SC1 SC2 SC3"
+    "Lu1b Iu1b0.A Iu1b1.V Qu1b Lx0 T00 CX00.A T01 CX01.A Lu1a Iu1a1.V Iu1a0.V Lu0a Iu0a0.A QX00 Iu0a1.V Lv2 "
+    "Iv20.A QX01 Qu1a Iv21.V M300 M301 Lu0b Iu0b0.V Qu0a Iu0b1.A Lv3 Iv30.V Iv31.A S300 S301 Qu0b M20 S20 M21 "
+    "S21 Lw1a Iw1a1.V Iw1a0.V Lx1 T10 T11 Lx2 T20 T21 CX10.A CX11.A CX20.A CX21.A P300 P301 Qv2 I30.V P20 QX10 "
+    "Lx3 T30 T31 Lw1b Iw1b1.A Qw1a QX20 P21 Qv3 Iw1b0.V M310 M311 S310 P310 M22 M23 CX30.A CX31.A QX30 M320 "
+    "S311 S320 S22 M24 M321 M25 M330 S23 S24 Qw1b QP30 P311 S321 S25 M26 M331 M27 P320 P22 P23 QP20 P24 P25 "
+    "P321 QP21 I31.A QP31 Lb S330 P330 MY0 A0 QP22 S331 I32.A QP32 P331 S26 S27 P26 P27 MY1 A1 MY2 MY3 MY4 MY5 "
+    "QP23 I33.A QP33 A2 A3 SY0 SY1 A4 A5 MY6 SY2 SY3 SY4 SY5 MY7 A6 SY6 A7 SY7 C0.A C1.A C2.A C3.A TY0 TY2 C4.A "
+    "C5.A TY4 C6.V TY6 C7.V CY0.A QY0 CY2.A CY4.A CY6.V QY1 TY7 CY7.A QY2 QY3 SC0 SC1 SC2 SC3"
 ).split(" ")
+NAMES = [s.split(".")[0] for s in ORDER]
 
 
 def tile_spamlowrankpolynomialorders_x1_kernel(tc, x, w1, u, lam, w, b, out_0, out_1, out_2):
@@ -49,10 +49,10 @@ def tile_spamlowrankpolynomialorders_x1_kernel(tc, x, w1, u, lam, w, b, out_0, o
         codes = {k: kept("codes_" + k, [P, 512], U32) for k in weights}
         scales = {k: kept("scales_" + k, [P, 512], U8) for k in weights}
         grouped = {}
-        x_rows = [kept("x_rows%d" % t, [P, D], BF16) for t in range(8)]
-        x_grouped = kept("x_grouped", [P, 2, 4 * N], BF16)
-        x_codes = kept("x_codes", [P, 2, N], U32)
-        x_scales = kept("x_scales", [P, 2, N], U8)
+        x_rows = [kept("x_rows%d" % t, [P, 2, D], BF16) for t in range(4)]
+        x_grouped = kept("x_grouped", [P, 4, 2048], BF16)
+        x_codes = kept("x_codes", [P, 4, 512], U32)
+        x_scales = kept("x_scales", [P, 4, 512], U8)
         p2 = kept("p2", [P, 4 * N], BF16)
         p3_rows = kept("p3_rows", [P, 4, 4, 256], BF16)
         p3 = kept("p3", [P, 4 * N], BF16)
@@ -93,20 +93,19 @@ def tile_spamlowrankpolynomialorders_x1_kernel(tc, x, w1, u, lam, w, b, out_0, o
             nc.tensor.matmul_mx(out=out, lhsT=lc.bitcast(FP8X4), lhsT_scale=ls, rhs=rc.bitcast(FP8X4),
                                 rhs_scale=rs, start=start, stop=stop)
 
-        def q_group(out, name, t, cols):
+        def q_group(out, name, t, q, c0, width):
             m = slice(128 * t, 128 * t + 128)
             for g in range(2):
                 k = name + "ab"[g]
-                mx(out, codes[k][:, m], scales[k][:, m], x_codes[:, g, cols], x_scales[:, g, cols], g == 0, g == 1)
+                cols = slice(256 * g + c0, 256 * g + c0 + width)
+                mx(out, codes[k][:, m], scales[k][:, m], x_codes[:, q, cols], x_scales[:, q, cols], g == 0, g == 1)
 
         def step(name, engine):
-            if name == "Llam":
-                nc.sync.dma_start(out=lam_sb[:], in_=lam.rearrange("o (p j) -> p o j", j=4))
-            elif name == "Lb":
+            if name == "Lb":
                 nc.sync.dma_start(out=bias[:], in_=b.partition_broadcast(P))
             elif name[0] == "L" and name[1] == "x":
                 t = int(name[2])
-                nc.sync.dma_start(out=x_rows[t][:], in_=x[128 * t : 128 * t + 128, :])
+                nc.sync.dma_start(out=x_rows[t][:], in_=x[256 * t : 256 * t + 256, :].rearrange("(a p) d -> p a d", a=2))
             elif name[0] == "L":
                 k = name[1:]
                 nc.sync.dma_start(out=raw[k][:], in_=weights[k].rearrange("(p j) c -> p j c", j=4))
@@ -119,17 +118,18 @@ def tile_spamlowrankpolynomialorders_x1_kernel(tc, x, w1, u, lam, w, b, out_0, o
                 if k not in grouped:
                     grouped[k] = rot.tile([P, 2048], BF16, name="grouped", tag="grouped", align_bytes=256)
                 if k[0] == "u":
-                    dst = grouped[k][:].rearrange("p (t a i j) -> p a t i j", t=4, i=2, j=4)
-                    src = raw[k][:].rearrange("p j (a i t) -> p a t i j", i=2, t=4)
-                    copy(engine, dst[:, :, 2 * h : 2 * h + 2], src[:, :, 2 * h : 2 * h + 2])
+                    dst = grouped[k][:].rearrange("p (t a i j) -> p a j i t", t=4, i=2, j=4)
+                    src = raw[k][:].rearrange("p j (a i t) -> p a j i t", i=2, t=4)
+                    copy(engine, dst[:, :, :, :, 2 * h : 2 * h + 2], src[:, :, :, :, 2 * h : 2 * h + 2])
                 else:
                     dst = grouped[k][:].rearrange("p (c i j) -> p c j i", i=4, j=4)
                     src = raw[k][:].rearrange("p j (c i) -> p c j i", i=4)
                     copy(engine, dst[:, 64 * h : 64 * h + 64], src[:, 64 * h : 64 * h + 64])
             elif name[:2] == "QX":
                 q, g = int(name[2]), int(name[3])
-                cols = slice(256 * q, 256 * q + 256)
-                quantize(x_codes[:, g, cols], x_scales[:, g, cols], x_grouped[:, g, 1024 * q : 1024 * q + 1024])
+                n = 1 if "QX%d1" % q in NAMES else 2
+                cols = slice(256 * g, 256 * (g + n))
+                quantize(x_codes[:, q, cols], x_scales[:, q, cols], x_grouped[:, q, 1024 * g : 1024 * (g + n)])
             elif name[:2] == "QP":
                 o, q = int(name[2]) - 2, int(name[3])
                 cols = slice(256 * q, 256 * q + 256)
@@ -149,38 +149,43 @@ def tile_spamlowrankpolynomialorders_x1_kernel(tc, x, w1, u, lam, w, b, out_0, o
             elif name[:2] == "TY":
                 t = int(name[2])
                 bank = new_bank(name)
-                words = y_bf[t][:].bitcast(F32)
-                for h in range(2):
-                    nc.tensor.transpose(bank[:, 128 * h : 128 * h + 128], words[:, h:256:2], ident[:])
+                n = 2 if t % 2 == 0 and "TY%d" % (t + 1) not in NAMES else 1
+                for a in range(n):
+                    words = y_bf[t + a][:].bitcast(F32)
+                    for h in range(2):
+                        c0 = 256 * a + 128 * h
+                        nc.tensor.transpose(bank[:, c0 : c0 + 128], words[:, 128 * h : 128 * h + 128], ident[:])
             elif name[0] == "T":
                 q, g = int(name[1]), int(name[2])
                 bank = new_bank(name)
                 for a in range(2):
-                    words = x_rows[2 * q + a][:].bitcast(F32)
+                    words = x_rows[q][:, a, :].bitcast(F32)
                     for h in range(2):
                         c0 = 128 * (2 * a + h)
                         nc.tensor.transpose(bank[:, c0 : c0 + 128], words[:, 256 * g + h : 256 * g + 256 : 2], ident[:])
             elif name[:2] == "CX":
                 q, g = int(name[2]), int(name[3])
-                dst = x_grouped[:, g, 1024 * q : 1024 * q + 1024].bitcast(F32).rearrange("p (a n h) -> p a n h", a=2, h=2)
+                dst = x_grouped[:, q, 1024 * g : 1024 * g + 1024].bitcast(F32).rearrange("p (a n h) -> p a n h", a=2, h=2)
                 copy(engine, dst, banks["T" + name[2:]][:].rearrange("p (a h n) -> p a n h", a=2, h=2))
             elif name[:2] == "CY":
                 t = int(name[2])
-                dst = y_grouped[:].bitcast(F32)[:, 256 * t : 256 * t + 256].rearrange("p (n h) -> p n h", h=2)
-                copy(engine, dst, banks["TY%d" % t][:, 0:256].rearrange("p (h n) -> p n h", h=2))
+                n = 2 if t % 2 == 0 and "TY%d" % (t + 1) not in NAMES else 1
+                dst = y_grouped[:, 512 * t : 512 * (t + n)].bitcast(F32).rearrange("p (a n h) -> p a n h", a=n, h=2)
+                copy(engine, dst, banks["TY%d" % t][:, 0 : 256 * n].rearrange("p (a h n) -> p a n h", a=n, h=2))
             elif name[0] == "C":
                 t = int(name[1])
-                copy(engine, y_bf[t][:], y[t][:])
+                copy(engine, y_bf[t][:].rearrange("p (h m e) -> p h m e", h=2, e=2),
+                     y[t][:].rearrange("p (m h e) -> p h m e", h=2, e=2))
             elif name[:2] == "M2":
                 t = int(name[2])
                 bank = new_bank(name)
                 for j in range(4):
-                    q_group(bank[:, 128 * j : 128 * j + 128], "u0", j, slice(128 * t, 128 * t + 128))
+                    q_group(bank[:, 128 * j : 128 * j + 128], "u0", j, t // 2, 128 * (t % 2), 128)
             elif name[:2] == "M3":
                 q, h = int(name[2]), int(name[3])
                 bank = new_bank(name)
                 for j in range(2):
-                    q_group(bank[:, 256 * j : 256 * j + 256], "u1", 2 * h + j, slice(256 * q, 256 * q + 256))
+                    q_group(bank[:, 256 * j : 256 * j + 256], "u1", 2 * h + j, q, 0, 256)
             elif name[:2] == "S2":
                 squares[name] = rot.tile([P, 512], F32, name="square", tag="square")
                 nc.scalar.activation(out=squares[name][:].rearrange("p (n j) -> p n j", j=4),
@@ -208,7 +213,8 @@ def tile_spamlowrankpolynomialorders_x1_kernel(tc, x, w1, u, lam, w, b, out_0, o
                 m = slice(128 * t, 128 * t + 128)
                 for g in range(2):
                     k = "w1" + "ab"[g]
-                    mx(bank[:], x_codes[:, g, m], x_scales[:, g, m], codes[k][:], scales[k][:], g == 0, False)
+                    xm = slice(256 * g + 128 * (t % 2), 256 * g + 128 * (t % 2) + 128)
+                    mx(bank[:], x_codes[:, t // 2, xm], x_scales[:, t // 2, xm], codes[k][:], scales[k][:], g == 0, False)
                 for o in range(2):
                     k = "v%d" % (o + 2)
                     mx(bank[:], p_codes[:, o, m], p_scales[:, o, m], codes[k][:], scales[k][:], False, o == 1)
@@ -223,6 +229,7 @@ def tile_spamlowrankpolynomialorders_x1_kernel(tc, x, w1, u, lam, w, b, out_0, o
                 cols = slice(256 * q, 256 * q + 256)
                 nc.sync.dma_start(out=out_words[:, cols], in_=y_codes[:, cols].bitcast(I32))
 
+        nc.gpsimd.dma_start(out=lam_sb[:], in_=lam.rearrange("o (p j) -> p o j", j=4))
         nc.gpsimd.memset(warm_in[:], 0.0)
         nc.scalar.activation(out=warm_out[:], in_=warm_in[:], func=SQUARE)
         make_identity(nc, ident[:])

@@ -18,15 +18,16 @@ SQUARE = mybir.ActivationFunctionType.Square
 
 P = 128
 ORDER = (
-    "Lu1b Iu1b0.A Iu1b1.V Qu1b Lx0 T00 CX00.A T01 CX01.A Lu1a Iu1a1.V Iu1a0.V Lu0a Iu0a0.A QX00 Iu0a1.V Lv2 "
-    "Iv20.A QX01 Qu1a Iv21.V M300 M301 Lu0b Iu0b0.V Qu0a Iu0b1.A Lv3 Iv30.V Iv31.A S300 S301 Qu0b M20 S20 M21 "
-    "S21 Lw1a Iw1a1.V Iw1a0.V Lx1 T10 T11 Lx2 T20 T21 CX10.A CX11.A CX20.A CX21.A P300 P301 Qv2 I30.V P20 QX10 "
-    "Lx3 T30 T31 Lw1b Iw1b1.A Qw1a QX20 P21 Qv3 Iw1b0.V M310 M311 S310 P310 M22 M23 CX30.A CX31.A QX30 M320 "
-    "S311 S320 S22 M24 M321 M25 M330 S23 S24 Qw1b QP30 P311 S321 S25 M26 M331 M27 P320 P22 P23 QP20 P24 P25 "
-    "P321 QP21 I31.A QP31 Lb S330 P330 MY0 A0 QP22 S331 I32.A QP32 P331 S26 S27 P26 P27 MY1 A1 MY2 MY3 MY4 MY5 "
-    "QP23 I33.A QP33 A2 A3 SY0 SY1 A4 A5 MY6 SY2 SY3 SY4 SY5 MY7 A6 SY6 A7 SY7 C0.A C1.A C2.A C3.A TY0 TY2 C4.A "
-    "C5.A TY4 C6.V TY6 C7.V CY0.A QY0 CY2.A CY4.A CY6.V QY1 TY7 CY7.A QY2 QY3 SC0 SC1 SC2 SC3"
+    "Lx0 Lu0b Iu0b1.V T00 CX00.V T01 Lu0a Iu0a0.V QX00 Iu0b0.A Qu0b Iu0a1.A Qu0a CX01.A QX01 Lx1 T10 T11 CX10.A "
+    "CX11.A Lu1b Iu1b0.V Iu1b1.V Lu1a Iu1a0.A Iu1a1.V Lw1b Iw1b1.A Iw1b0.A M20 M21 QX10 M22 M23 Qu1b Qu1a S20.V "
+    "S21.V P20 S22.V P21 M300 S300 P22 M301 M310 S23.A S301 S310 P300 P301 P310 Lw1a Iw1a1.G Lx2 Lv2 Lx3 T20 "
+    "CX20.A T21 CX21.A T30 T31 CX30.A CX31.A QP20 QX20 Qw1b Iv20.V QX30 Lv3 Iv31.A Iv30.A Iw1a0.G Iv21.G P23 "
+    "Qw1a Qv3 Qv2 M311 M320 M321 M24 M330 M331 I30.A QP30 S311 QP21 P311 S320 S321 S330 S331 P320 P321 P330 "
+    "P331 I31.G QP31 S24.A M25 S25.A P24 P25 MY0 M26 M27 MY1 MY2 Lb A0 SY0 I32.A QP32 QP22 MY3 MY4 MY5 S26.A "
+    "P26 S27.A P27 A1 SY1 I33.A QP33 QP23 A2 A3 A4 A5 SY2 SY3 SY4 SY5 MY6 MY7 A6 SY6 A7 SY7 C0.A C1.A C2.A TY0 "
+    "C3.A C4.G C5.A C6.V C7.V CY0.A QY0 TY2 CY2.A TY4 TY6 CY4.A TY7 CY6.V CY7.A QY1 QY2 SC0 SC1 SC2 QY3 SC3"
 ).split(" ")
+SHARES = {"w1a": "u1a"}
 NAMES = [s.split(".")[0] for s in ORDER]
 
 
@@ -86,6 +87,12 @@ def tile_spamlowrankpolynomialorders_x1_kernel(tc, x, w1, u, lam, w, b, out_0, o
             else:
                 nc.gpsimd.tensor_scalar(out=out, in0=in_, scalar1=1.0, scalar2=0.0, op0=MULT, op1=ADD)
 
+        def interleave(engine, out, in_):
+            if engine == "G":
+                copy(engine, out.rearrange("p (c j) -> p c j", j=4), in_.rearrange("p j c -> p c j"))
+            else:
+                copy(engine, out.rearrange("p (c i j) -> p c j i", i=4, j=4), in_.rearrange("p j (c i) -> p c j i", i=4))
+
         def quantize(cds, scl, in_):
             nc.vector.quantize_mx(out=cds.bitcast(FP8X4), scales=scl, in_=in_)
 
@@ -111,20 +118,18 @@ def tile_spamlowrankpolynomialorders_x1_kernel(tc, x, w1, u, lam, w, b, out_0, o
                 nc.sync.dma_start(out=raw[k][:], in_=weights[k].rearrange("(p j) c -> p j c", j=4))
             elif name[:2] == "I3":
                 q = int(name[2])
-                dst = p3[:, 1024 * q : 1024 * q + 1024].rearrange("p (c i j) -> p c j i", i=4, j=4)
-                copy(engine, dst, p3_rows[:, q, :, :].rearrange("p j (c i) -> p c j i", i=4))
+                interleave(engine, p3[:, 1024 * q : 1024 * q + 1024], p3_rows[:, q, :, :])
             elif name[0] == "I":
                 k, h = name[1:-1], int(name[-1])
                 if k not in grouped:
-                    grouped[k] = rot.tile([P, 2048], BF16, name="grouped", tag="grouped", align_bytes=256)
+                    tag = "grouped_" + SHARES.get(k, k)
+                    grouped[k] = keep.tile([P, 2048], BF16, name=tag, tag=tag, align_bytes=256)
                 if k[0] == "u":
                     dst = grouped[k][:].rearrange("p (t a i j) -> p a j i t", t=4, i=2, j=4)
                     src = raw[k][:].rearrange("p j (a i t) -> p a j i t", i=2, t=4)
                     copy(engine, dst[:, :, :, :, 2 * h : 2 * h + 2], src[:, :, :, :, 2 * h : 2 * h + 2])
                 else:
-                    dst = grouped[k][:].rearrange("p (c i j) -> p c j i", i=4, j=4)
-                    src = raw[k][:].rearrange("p j (c i) -> p c j i", i=4)
-                    copy(engine, dst[:, 64 * h : 64 * h + 64], src[:, 64 * h : 64 * h + 64])
+                    interleave(engine, grouped[k][:, 1024 * h : 1024 * h + 1024], raw[k][:, :, 256 * h : 256 * h + 256])
             elif name[:2] == "QX":
                 q, g = int(name[2]), int(name[3])
                 n = 1 if "QX%d1" % q in NAMES else 2
@@ -188,8 +193,12 @@ def tile_spamlowrankpolynomialorders_x1_kernel(tc, x, w1, u, lam, w, b, out_0, o
                     q_group(bank[:, 256 * j : 256 * j + 256], "u1", 2 * h + j, q, 0, 256)
             elif name[:2] == "S2":
                 squares[name] = rot.tile([P, 512], F32, name="square", tag="square")
-                nc.scalar.activation(out=squares[name][:].rearrange("p (n j) -> p n j", j=4),
-                                     in_=banks["M2" + name[2:]][:].rearrange("p (j n) -> p n j", j=4), func=SQUARE)
+                dst = squares[name][:].rearrange("p (n j) -> p n j", j=4)
+                src = banks["M2" + name[2:]][:].rearrange("p (j n) -> p n j", j=4)
+                if engine == "V":
+                    nc.vector.tensor_tensor(out=dst, in0=src, in1=lam_sb[:, 0, :].unsqueeze(1).to_broadcast([P, 128, 4]), op=MULT)
+                else:
+                    nc.scalar.activation(out=dst, in_=src, func=SQUARE)
             elif name[:2] == "S3":
                 squares[name] = rot.tile([P, 512], F32, name="square", tag="square")
                 nc.scalar.activation(out=squares[name][:], in_=banks["M3" + name[2:]][:], func=SQUARE)
@@ -198,7 +207,8 @@ def tile_spamlowrankpolynomialorders_x1_kernel(tc, x, w1, u, lam, w, b, out_0, o
                 nc.vector.tensor_tensor(
                     out=p2[:, 512 * t : 512 * t + 512].rearrange("p (n j) -> p n j", j=4),
                     in0=squares["S2%d" % t][:].rearrange("p (n j) -> p n j", j=4),
-                    in1=lam_sb[:, 0, :].unsqueeze(1).to_broadcast([P, 128, 4]), op=MULT)
+                    in1=banks["M2%d" % t][:].rearrange("p (j n) -> p n j", j=4) if "S2%d.V" % t in ORDER
+                    else lam_sb[:, 0, :].unsqueeze(1).to_broadcast([P, 128, 4]), op=MULT)
             elif name[:2] == "P3":
                 q, h = int(name[2]), int(name[3])
                 for j in range(2):

@@ -17,236 +17,365 @@ ADD = mybir.AluOpType.add
 SQUARE = mybir.ActivationFunctionType.Square
 
 P = 128
-ORDER = (
-    "Lx0 Lu0b Iu0b1.V T00 CX00.V T01 Lu0a Iu0a0.V QX00 Iu0b0.A Qu0b Iu0a1.A Qu0a CX01.A QX01 Lx1 T10 T11 CX10.A "
-    "CX11.A Lu1b Iu1b0.V Iu1b1.V Lu1a Iu1a0.A Iu1a1.V Lw1b Iw1b1.A Iw1b0.A M20 M21 QX10 M22 M23 Qu1b Qu1a S20.V "
-    "S21.V P20 S22.V P21 M300 S300 P22 M301 M310 S23.A S301 S310 P300 P301 P310 Lw1a Iw1a1.G Lx2 Lv2 Lx3 T20 "
-    "CX20.A T21 CX21.A T30 T31 CX30.A CX31.A QP20 QX20 Qw1b Iv20.V QX30 Lv3 Iv31.A Iv30.A Iw1a0.G Iv21.G P23 "
-    "Qw1a Qv3 Qv2 M311 M320 M321 M24 M330 M331 I30.A QP30 S311 QP21 P311 S320 S321 S330 S331 P320 P321 P330 "
-    "P331 I31.G QP31 S24.A M25 S25.A P24 P25 MY0 M26 M27 MY1 MY2 Lb A0 SY0 I32.A QP32 QP22 MY3 MY4 MY5 S26.A "
-    "P26 S27.A P27 A1 SY1 I33.A QP33 QP23 A2 A3 A4 A5 SY2 SY3 SY4 SY5 MY6 MY7 A6 SY6 A7 SY7 C0.A C1.A C2.A TY0 "
-    "C3.A C4.G C5.A C6.V C7.V CY0.A QY0 TY2 CY2.A TY4 TY6 CY4.A TY7 CY6.V CY7.A QY1 QY2 SC0 SC1 SC2 QY3 SC3"
-).split(" ")
-SHARES = {"w1a": "u1a"}
-NAMES = [s.split(".")[0] for s in ORDER]
+SLOTS = 4
+K_PASS = P * SLOTS
+QUARTER = 2 * P
+TILES, QUARTERS = N // P, N // QUARTER
+BANKS, BANK_WORDS = 8, 512
+ALIGN = 256
+FIRST_FACTOR_BUFS = 8
+
+
+def span(index, width):
+    return slice(index * width, (index + 1) * width)
 
 
 def tile_spamlowrankpolynomialorders_x1_kernel(tc, x, w1, u, lam, w, b, out_0, out_1, out_2):
     nc = tc.nc
     with ExitStack() as ctx:
         keep = ctx.enter_context(tc.tile_pool(name="keep", bufs=1))
-        rot = ctx.enter_context(tc.tile_pool(name="rot", bufs=8))
+        factors = ctx.enter_context(tc.tile_pool(name="factors", bufs=FIRST_FACTOR_BUFS))
         psum = ctx.enter_context(tc.psum_pool(name="psum", bufs=1))
         ctx.enter_context(tc.manual_schedule())
 
         def kept(name, shape, dtype):
-            return keep.tile(shape, dtype, name=name, align_bytes=256)
+            return keep.tile(shape, dtype, name=name, tag=name, align_bytes=ALIGN)
 
-        weights = {
-            "u0a": u[0, 0:512, :], "u0b": u[0, 512:1024, :], "u1a": u[1, 0:512, :], "u1b": u[1, 512:1024, :],
-            "w1a": w1[0:512, :], "w1b": w1[512:1024, :], "v2": w[0], "v3": w[1],
-        }
-        raw = {k: kept("raw_" + k, [P, 4, 512], BF16) for k in weights}
-        codes = {k: kept("codes_" + k, [P, 512], U32) for k in weights}
-        scales = {k: kept("scales_" + k, [P, 512], U8) for k in weights}
-        grouped = {}
-        x_rows = [kept("x_rows%d" % t, [P, 2, D], BF16) for t in range(4)]
-        x_grouped = kept("x_grouped", [P, 4, 2048], BF16)
-        x_codes = kept("x_codes", [P, 4, 512], U32)
-        x_scales = kept("x_scales", [P, 4, 512], U8)
-        p2 = kept("p2", [P, 4 * N], BF16)
-        p3_rows = kept("p3_rows", [P, 4, 4, 256], BF16)
-        p3 = kept("p3", [P, 4 * N], BF16)
-        p_codes = kept("p_codes", [P, 2, N], U32)
-        p_scales = kept("p_scales", [P, 2, N], U8)
-        y = [kept("y%d" % t, [P, C], F32) for t in range(8)]
-        y_bf = [kept("y_bf%d" % t, [P, C], BF16) for t in range(8)]
-        y_grouped = kept("y_grouped", [P, 4 * N], BF16)
+        weights = {}
+        for g in range(D // K_PASS):
+            weights["u2", g] = u[0, span(g, K_PASS), :]
+            weights["u3", g] = u[1, span(g, K_PASS), :]
+            weights["w1", g] = w1[span(g, K_PASS), :]
+        weights["w2", 0] = w[0]
+        weights["w3", 0] = w[1]
+        rows = {key: kept("rows_%s_%d" % key, [P, SLOTS, 512], BF16) for key in weights}
+        codes = {key: kept("codes_%s_%d" % key, [P, 512], U32) for key in weights}
+        scales = {key: kept("scales_%s_%d" % key, [P, 512], U8) for key in weights}
+        staged = {}
+
+        x_rows = [kept("x_rows%d" % q, [P, 2, D], BF16) for q in range(QUARTERS)]
+        x_staged = kept("x_staged", [P, QUARTERS, 2 * QUARTER * SLOTS], BF16)
+        x_codes = kept("x_codes", [P, QUARTERS, 2 * QUARTER], U32)
+        x_scales = kept("x_scales", [P, QUARTERS, 2 * QUARTER], U8)
+        p3_rows = kept("p3_rows", [P, QUARTERS, SLOTS, QUARTER], BF16)
+        p_staged = {order: kept("p%d_staged" % order, [P, N * SLOTS], BF16) for order in (2, 3)}
+        p_codes = {order: kept("p%d_codes" % order, [P, N], U32) for order in (2, 3)}
+        p_scales = {order: kept("p%d_scales" % order, [P, N], U8) for order in (2, 3)}
+        y = [kept("y%d" % i, [P, C], F32) for i in range(TILES)]
+        y_rounded = [kept("y_rounded%d" % i, [P, C], BF16) for i in range(TILES)]
+        y_staged = kept("y_staged", [P, N * SLOTS], BF16)
         y_codes = kept("y_codes", [P, N], U32)
         y_scales = kept("y_scales", [P, N], U8)
-        ident = kept("ident", [P, P], F32)
-        lam_sb = kept("lam_sb", [P, 2, 4], BF16)
+        mask = kept("mask", [P, P], F32)
+        identity = kept("identity", [P, P], F32)
+        lam_sb = kept("lam_sb", [P, 2, SLOTS], BF16)
         bias = kept("bias", [P, C], BF16)
-        warm_in = kept("warm_in", [P, 1], F32)
-        warm_out = kept("warm_out", [P, 1], F32)
-        banks = {}
-        squares = {}
-        out_words = out_1[0].rearrange("p m t -> p (m t)").bitcast(I32)
+        lam2_by_token = lam_sb[:, 0, :].unsqueeze(1).to_broadcast([P, P, SLOTS])
+        out_words = out_1[0].rearrange("p n j -> p (n j)").bitcast(I32)
         out_scales = out_2[0].bitcast(I32)
+        banks = {}
+        first_factor = {}
+        second_factor = {}
 
         def new_bank(key):
-            i = len(banks) % 8
-            banks[key] = psum.tile([P, 512], F32, name="bank%d" % i, tag="bank%d" % i)
+            name = "bank%d" % (len(banks) % BANKS)
+            banks[key] = psum.tile([P, BANK_WORDS], F32, name=name, tag=name)
             return banks[key]
 
-        def copy(engine, out, in_):
-            if engine == "A":
-                nc.scalar.copy(out=out, in_=in_)
-            elif engine == "V":
-                nc.vector.tensor_copy(out=out, in_=in_)
+        def on_vector(out, in_):
+            nc.vector.tensor_copy(out=out, in_=in_)
+
+        def on_scalar(out, in_):
+            nc.scalar.copy(out=out, in_=in_)
+
+        def on_gpsimd(out, in_):
+            nc.gpsimd.tensor_scalar(out=out, in0=in_, scalar1=1.0, scalar2=0.0, op0=MULT, op1=ADD)
+
+        def quantize(words, scale_bytes, in_):
+            nc.vector.quantize_mx(out=words.bitcast(FP8X4), scales=scale_bytes, in_=in_)
+
+        def multiply(out, passes):
+            for index, (lhs_words, lhs_scales, rhs_words, rhs_scales) in enumerate(passes):
+                nc.tensor.matmul_mx(
+                    out=out,
+                    lhsT=lhs_words.bitcast(FP8X4),
+                    lhsT_scale=lhs_scales,
+                    rhs=rhs_words.bitcast(FP8X4),
+                    rhs_scale=rhs_scales,
+                    start=index == 0,
+                    stop=index == len(passes) - 1,
+                )
+
+        def interleave(copy, out, in_, run):
+            copy(
+                out.rearrange("p (c col j) -> p c j col", col=run, j=SLOTS),
+                in_.rearrange("p j (c col) -> p c j col", col=run),
+            )
+
+        def load_weight(key):
+            nc.sync.dma_start(out=rows[key][:], in_=weights[key].rearrange("(p j) c -> p j c", j=SLOTS))
+
+        def staged_tile(key, tag):
+            if key not in staged:
+                staged[key] = kept("staged_%s_%d" % tag, [P, 512 * SLOTS], BF16)
+            return staged[key]
+
+        def interleave_u(key, half, copy):
+            out = staged_tile(key, key)[:]
+            out = out.rearrange("p (s line odd j) -> p line j odd s", s=SLOTS, odd=2, j=SLOTS)
+            in_ = rows[key][:].rearrange("p j (line odd s) -> p line j odd s", odd=2, s=SLOTS)
+            copy(out[:, :, :, :, span(half, 2)], in_[:, :, :, :, span(half, 2)])
+
+        def interleave_w(key, first, last, copy, run, tag=None):
+            out = staged_tile(key, tag or key)[:, SLOTS * first : SLOTS * last]
+            interleave(copy, out, rows[key][:, :, first:last], run)
+
+        def quantize_weight(key):
+            quantize(codes[key][:], scales[key][:], staged[key][:])
+
+        def load_x(q):
+            nc.sync.dma_start(out=x_rows[q][:], in_=x[span(q, QUARTER), :].rearrange("(a n) d -> n a d", a=2))
+
+        def transpose_x(q, g):
+            bank = new_bank(("x", q, g))
+            for a in range(2):
+                words = x_rows[q][:, a, :].bitcast(F32)[:, span(g, K_PASS // 2)]
+                for h in range(2):
+                    nc.tensor.transpose(bank[:, span(2 * a + h, P)], words[:, h : K_PASS // 2 : 2], identity[:])
+
+        def copy_words(copy, out, bank_part):
+            copy(
+                out.bitcast(F32).rearrange("p (a n h) -> p a n h", n=P, h=2),
+                bank_part.rearrange("p (a h n) -> p a n h", h=2, n=P),
+            )
+
+        def stage_x(q, g, copy):
+            copy_words(copy, x_staged[:, q, span(g, QUARTER * SLOTS)], banks["x", q, g][:])
+
+        def quantize_x(q, first, last):
+            columns = slice(QUARTER * first, QUARTER * last)
+            in_ = x_staged[:, q, QUARTER * SLOTS * first : QUARTER * SLOTS * last]
+            quantize(x_codes[:, q, columns], x_scales[:, q, columns], in_)
+
+        def x_operand(g, first_token, tokens):
+            q, offset = divmod(first_token, QUARTER)
+            columns = slice(QUARTER * g + offset, QUARTER * g + offset + tokens)
+            return x_codes[:, q, columns], x_scales[:, q, columns]
+
+        def project(out, name, j, first_token, tokens):
+            multiply(out, [
+                (codes[name, g][:, span(j, P)], scales[name, g][:, span(j, P)]) + x_operand(g, first_token, tokens)
+                for g in range(D // K_PASS)
+            ])
+
+        def project2(i):
+            bank = new_bank(("q2", i))
+            for j in range(SLOTS):
+                project(bank[:, span(j, P)], "u2", j, P * i, P)
+
+        def begin_p2(i, scalar_squares):
+            factor = factors.tile([P, P, SLOTS], F32, name="factor", tag="factor")
+            q2 = banks["q2", i][:].rearrange("p (j n) -> p n j", j=SLOTS)
+            if scalar_squares:
+                nc.scalar.activation(out=factor[:], in_=q2, func=SQUARE)
             else:
-                nc.gpsimd.tensor_scalar(out=out, in0=in_, scalar1=1.0, scalar2=0.0, op0=MULT, op1=ADD)
+                nc.vector.tensor_tensor(out=factor[:], in0=q2, in1=lam2_by_token, op=MULT)
+            first_factor[2, i] = factor
+            second_factor[i] = lam2_by_token if scalar_squares else q2
 
-        def interleave(engine, out, in_):
-            if engine == "G":
-                copy(engine, out.rearrange("p (c j) -> p c j", j=4), in_.rearrange("p j c -> p c j"))
-            else:
-                copy(engine, out.rearrange("p (c i j) -> p c j i", i=4, j=4), in_.rearrange("p j (c i) -> p c j i", i=4))
+        def finish_p2(i):
+            out = p_staged[2][:, span(i, P * SLOTS)].rearrange("p (n j) -> p n j", j=SLOTS)
+            nc.vector.tensor_tensor(out=out, in0=first_factor[2, i][:], in1=second_factor[i], op=MULT)
 
-        def quantize(cds, scl, in_):
-            nc.vector.quantize_mx(out=cds.bitcast(FP8X4), scales=scl, in_=in_)
+        def project3(q, half):
+            bank = new_bank(("q3", q, half))
+            for j in (2 * half, 2 * half + 1):
+                project(bank[:, span(j % 2, QUARTER)], "u3", j, QUARTER * q, QUARTER)
 
-        def mx(out, lc, ls, rc, rs, start, stop):
-            nc.tensor.matmul_mx(out=out, lhsT=lc.bitcast(FP8X4), lhsT_scale=ls, rhs=rc.bitcast(FP8X4),
-                                rhs_scale=rs, start=start, stop=stop)
+        def begin_p3(q, half):
+            factor = factors.tile([P, BANK_WORDS], F32, name="factor", tag="factor")
+            nc.scalar.activation(out=factor[:], in_=banks["q3", q, half][:], func=SQUARE)
+            first_factor[3, q, half] = factor
 
-        def q_group(out, name, t, q, c0, width):
-            m = slice(128 * t, 128 * t + 128)
+        def finish_p3(q, half):
+            for j in (2 * half, 2 * half + 1):
+                nc.vector.scalar_tensor_tensor(
+                    out=p3_rows[:, q, j, :],
+                    in0=first_factor[3, q, half][:, span(j % 2, QUARTER)],
+                    scalar=lam_sb[:, 1, j : j + 1],
+                    in1=banks["q3", q, half][:, span(j % 2, QUARTER)],
+                    op0=MULT,
+                    op1=MULT,
+                )
+
+        def interleave_p3(q, copy, run):
+            interleave(copy, p_staged[3][:, span(q, QUARTER * SLOTS)], p3_rows[:, q, :, :], run)
+
+        def quantize_p(order, q):
+            columns = span(q, QUARTER)
+            in_ = p_staged[order][:, span(q, QUARTER * SLOTS)]
+            quantize(p_codes[order][:, columns], p_scales[order][:, columns], in_)
+
+        def sum_terms(i):
+            linear = [x_operand(g, P * i, P) + (codes["w1", g][:], scales["w1", g][:]) for g in range(D // K_PASS)]
+            powers = [
+                (p_codes[order][:, span(i, P)], p_scales[order][:, span(i, P)], codes[name, 0][:], scales[name, 0][:])
+                for order, name in ((2, "w2"), (3, "w3"))
+            ]
+            multiply(new_bank(("y", i))[:], linear + powers)
+
+        def store_y(i):
+            nc.vector.tensor_tensor(out=y[i][:], in0=banks["y", i][:], in1=bias[:], op=ADD)
+            nc.sync.dma_start(out=out_0[span(i, P), :], in_=y[i][:])
+
+        def round_y(i, copy):
+            copy(
+                y_rounded[i][:].rearrange("p (h m e) -> p h m e", h=2, e=2),
+                y[i][:].rearrange("p (m h e) -> p h m e", h=2, e=2),
+            )
+
+        def transpose_y(first, last):
+            bank = new_bank(("yt", first))
+            for i in range(first, last):
+                words = y_rounded[i][:].bitcast(F32)
+                for h in range(2):
+                    nc.tensor.transpose(bank[:, span(2 * (i - first) + h, P)], words[:, span(h, P)], identity[:])
+
+        def stage_y(first, last, copy):
+            out = y_staged[:, P * SLOTS * first : P * SLOTS * last]
+            copy_words(copy, out, banks["yt", first][:, : 2 * P * (last - first)])
+
+        def store_planes(q):
+            columns = span(q, QUARTER)
+            quantize(y_codes[:, columns], y_scales[:, columns], y_staged[:, span(q, QUARTER * SLOTS)])
+            nc.sync.dma_start(out=out_words[:, columns], in_=y_codes[:, columns].bitcast(I32))
+
+        long_run, short_run = 4, 1
+
+        make_identity(nc, mask[:])
+        nc.scalar.activation(out=identity[:], in_=mask[:], func=SQUARE)
+        nc.gpsimd.dma_start(out=lam_sb[:], in_=lam.rearrange("o (p j) -> p o j", j=SLOTS))
+
+        for q, keys in enumerate(([("u2", 0), ("u2", 1)], [("u3", 0), ("u3", 1), ("w1", 0), ("w1", 1)],
+                                  [("w2", 0)], [("w3", 0)])):
+            load_x(q)
+            for key in keys:
+                load_weight(key)
+        nc.sync.dma_start(out=bias[:], in_=b.partition_broadcast(P))
+
+        for q in range(2):
             for g in range(2):
-                k = name + "ab"[g]
-                cols = slice(256 * g + c0, 256 * g + c0 + width)
-                mx(out, codes[k][:, m], scales[k][:, m], x_codes[:, q, cols], x_scales[:, q, cols], g == 0, g == 1)
+                transpose_x(q, g)
+        interleave_u(("u2", 0), 0, on_scalar)
+        interleave_u(("u2", 0), 1, on_vector)
+        stage_x(0, 0, on_vector)
+        interleave_u(("u2", 1), 0, on_vector)
+        interleave_u(("u2", 1), 1, on_scalar)
+        stage_x(0, 1, on_scalar)
+        quantize_x(0, 0, 1)
+        quantize_weight(("u2", 0))
+        quantize_weight(("u2", 1))
+        quantize_x(0, 1, 2)
+        for g in range(2):
+            stage_x(1, g, on_scalar)
+        for half in range(2):
+            interleave_u(("u3", 0), half, on_vector)
+        interleave_u(("u3", 1), 0, on_scalar)
+        interleave_u(("u3", 1), 1, on_vector)
+        quantize_x(1, 0, 2)
+        quantize_weight(("u3", 0))
+        quantize_weight(("u3", 1))
 
-        def step(name, engine):
-            if name == "Lb":
-                nc.sync.dma_start(out=bias[:], in_=b.partition_broadcast(P))
-            elif name[0] == "L" and name[1] == "x":
-                t = int(name[2])
-                nc.sync.dma_start(out=x_rows[t][:], in_=x[256 * t : 256 * t + 256, :].rearrange("(a p) d -> p a d", a=2))
-            elif name[0] == "L":
-                k = name[1:]
-                nc.sync.dma_start(out=raw[k][:], in_=weights[k].rearrange("(p j) c -> p j c", j=4))
-            elif name[:2] == "I3":
-                q = int(name[2])
-                interleave(engine, p3[:, 1024 * q : 1024 * q + 1024], p3_rows[:, q, :, :])
-            elif name[0] == "I":
-                k, h = name[1:-1], int(name[-1])
-                if k not in grouped:
-                    tag = "grouped_" + SHARES.get(k, k)
-                    grouped[k] = keep.tile([P, 2048], BF16, name=tag, tag=tag, align_bytes=256)
-                if k[0] == "u":
-                    dst = grouped[k][:].rearrange("p (t a i j) -> p a j i t", t=4, i=2, j=4)
-                    src = raw[k][:].rearrange("p j (a i t) -> p a j i t", i=2, t=4)
-                    copy(engine, dst[:, :, :, :, 2 * h : 2 * h + 2], src[:, :, :, :, 2 * h : 2 * h + 2])
-                else:
-                    interleave(engine, grouped[k][:, 1024 * h : 1024 * h + 1024], raw[k][:, :, 256 * h : 256 * h + 256])
-            elif name[:2] == "QX":
-                q, g = int(name[2]), int(name[3])
-                n = 1 if "QX%d1" % q in NAMES else 2
-                cols = slice(256 * g, 256 * (g + n))
-                quantize(x_codes[:, q, cols], x_scales[:, q, cols], x_grouped[:, q, 1024 * g : 1024 * (g + n)])
-            elif name[:2] == "QP":
-                o, q = int(name[2]) - 2, int(name[3])
-                cols = slice(256 * q, 256 * q + 256)
-                quantize(p_codes[:, o, cols], p_scales[:, o, cols], (p2, p3)[o][:, 1024 * q : 1024 * q + 1024])
-            elif name[:2] == "QY":
-                q = int(name[2])
-                cols = slice(256 * q, 256 * q + 256)
-                quantize(y_codes[:, cols], y_scales[:, cols], y_grouped[:, 1024 * q : 1024 * q + 1024])
-            elif name[0] == "Q":
-                if name[1:] in weights:
-                    k = name[1:]
-                    quantize(codes[k][:], scales[k][:], grouped[k][:])
-                else:
-                    k, h = name[1:-1], int(name[-1])
-                    cols = slice(256 * h, 256 * h + 256)
-                    quantize(codes[k][:, cols], scales[k][:, cols], grouped[k][:, 1024 * h : 1024 * h + 1024])
-            elif name[:2] == "TY":
-                t = int(name[2])
-                bank = new_bank(name)
-                n = 2 if t % 2 == 0 and "TY%d" % (t + 1) not in NAMES else 1
-                for a in range(n):
-                    words = y_bf[t + a][:].bitcast(F32)
-                    for h in range(2):
-                        c0 = 256 * a + 128 * h
-                        nc.tensor.transpose(bank[:, c0 : c0 + 128], words[:, 128 * h : 128 * h + 128], ident[:])
-            elif name[0] == "T":
-                q, g = int(name[1]), int(name[2])
-                bank = new_bank(name)
-                for a in range(2):
-                    words = x_rows[q][:, a, :].bitcast(F32)
-                    for h in range(2):
-                        c0 = 128 * (2 * a + h)
-                        nc.tensor.transpose(bank[:, c0 : c0 + 128], words[:, 256 * g + h : 256 * g + 256 : 2], ident[:])
-            elif name[:2] == "CX":
-                q, g = int(name[2]), int(name[3])
-                dst = x_grouped[:, q, 1024 * g : 1024 * g + 1024].bitcast(F32).rearrange("p (a n h) -> p a n h", a=2, h=2)
-                copy(engine, dst, banks["T" + name[2:]][:].rearrange("p (a h n) -> p a n h", a=2, h=2))
-            elif name[:2] == "CY":
-                t = int(name[2])
-                n = 2 if t % 2 == 0 and "TY%d" % (t + 1) not in NAMES else 1
-                dst = y_grouped[:, 512 * t : 512 * (t + n)].bitcast(F32).rearrange("p (a n h) -> p a n h", a=n, h=2)
-                copy(engine, dst, banks["TY%d" % t][:, 0 : 256 * n].rearrange("p (a h n) -> p a n h", a=n, h=2))
-            elif name[0] == "C":
-                t = int(name[1])
-                copy(engine, y_bf[t][:].rearrange("p (h m e) -> p h m e", h=2, e=2),
-                     y[t][:].rearrange("p (m h e) -> p h m e", h=2, e=2))
-            elif name[:2] == "M2":
-                t = int(name[2])
-                bank = new_bank(name)
-                for j in range(4):
-                    q_group(bank[:, 128 * j : 128 * j + 128], "u0", j, t // 2, 128 * (t % 2), 128)
-            elif name[:2] == "M3":
-                q, h = int(name[2]), int(name[3])
-                bank = new_bank(name)
-                for j in range(2):
-                    q_group(bank[:, 256 * j : 256 * j + 256], "u1", 2 * h + j, q, 0, 256)
-            elif name[:2] == "S2":
-                squares[name] = rot.tile([P, 512], F32, name="square", tag="square")
-                dst = squares[name][:].rearrange("p (n j) -> p n j", j=4)
-                src = banks["M2" + name[2:]][:].rearrange("p (j n) -> p n j", j=4)
-                if engine == "V":
-                    nc.vector.tensor_tensor(out=dst, in0=src, in1=lam_sb[:, 0, :].unsqueeze(1).to_broadcast([P, 128, 4]), op=MULT)
-                else:
-                    nc.scalar.activation(out=dst, in_=src, func=SQUARE)
-            elif name[:2] == "S3":
-                squares[name] = rot.tile([P, 512], F32, name="square", tag="square")
-                nc.scalar.activation(out=squares[name][:], in_=banks["M3" + name[2:]][:], func=SQUARE)
-            elif name[:2] == "P2":
-                t = int(name[2])
-                nc.vector.tensor_tensor(
-                    out=p2[:, 512 * t : 512 * t + 512].rearrange("p (n j) -> p n j", j=4),
-                    in0=squares["S2%d" % t][:].rearrange("p (n j) -> p n j", j=4),
-                    in1=banks["M2%d" % t][:].rearrange("p (j n) -> p n j", j=4) if "S2%d.V" % t in ORDER
-                    else lam_sb[:, 0, :].unsqueeze(1).to_broadcast([P, 128, 4]), op=MULT)
-            elif name[:2] == "P3":
-                q, h = int(name[2]), int(name[3])
-                for j in range(2):
-                    cols = slice(256 * j, 256 * j + 256)
-                    t = 2 * h + j
-                    nc.vector.scalar_tensor_tensor(
-                        out=p3_rows[:, q, t, :], in0=squares["S3" + name[2:]][:, cols], scalar=lam_sb[:, 1, t : t + 1],
-                        in1=banks["M3" + name[2:]][:, cols], op0=MULT, op1=MULT)
-            elif name[:2] == "MY":
-                t = int(name[2])
-                bank = new_bank(name)
-                m = slice(128 * t, 128 * t + 128)
-                for g in range(2):
-                    k = "w1" + "ab"[g]
-                    xm = slice(256 * g + 128 * (t % 2), 256 * g + 128 * (t % 2) + 128)
-                    mx(bank[:], x_codes[:, t // 2, xm], x_scales[:, t // 2, xm], codes[k][:], scales[k][:], g == 0, False)
-                for o in range(2):
-                    k = "v%d" % (o + 2)
-                    mx(bank[:], p_codes[:, o, m], p_scales[:, o, m], codes[k][:], scales[k][:], False, o == 1)
-            elif name[0] == "A":
-                t = int(name[1])
-                nc.vector.tensor_tensor(out=y[t][:], in0=banks["MY%d" % t][:], in1=bias[:], op=ADD)
-            elif name[:2] == "SY":
-                t = int(name[2])
-                nc.sync.dma_start(out=out_0[128 * t : 128 * t + 128, :], in_=y[t][:])
-            else:
-                q = int(name[2])
-                cols = slice(256 * q, 256 * q + 256)
-                nc.sync.dma_start(out=out_words[:, cols], in_=y_codes[:, cols].bitcast(I32))
+        early_p3 = [(0, 0), (0, 1), (1, 0)]
+        for i in range(4):
+            project2(i)
+        for q, half in early_p3:
+            project3(q, half)
+        interleave_w(("w1", 0), 0, C, on_scalar, long_run)
+        interleave_w(("w1", 1), 0, C, on_gpsimd, short_run, tag=("u3", 1))
+        interleave_w(("w2", 0), 0, C // 2, on_gpsimd, short_run)
+        begin_p2(0, False)
+        for i in range(1, 3):
+            begin_p2(i, False)
+            finish_p2(i - 1)
+        finish_p2(2)
+        begin_p3(0, 0)
+        begin_p2(3, True)
+        for q, half in early_p3[1:]:
+            begin_p3(q, half)
+        for q, half in early_p3:
+            finish_p3(q, half)
+        for q in range(2, QUARTERS):
+            for g in range(2):
+                transpose_x(q, g)
+        for q in range(2, QUARTERS):
+            for g in range(2):
+                stage_x(q, g, on_scalar)
+        project3(1, 1)
 
-        nc.gpsimd.dma_start(out=lam_sb[:], in_=lam.rearrange("o (p j) -> p o j", j=4))
-        nc.gpsimd.memset(warm_in[:], 0.0)
-        nc.scalar.activation(out=warm_out[:], in_=warm_in[:], func=SQUARE)
-        make_identity(nc, ident[:])
-        for s in ORDER:
-            parts = s.split(".")
-            step(parts[0], parts[-1])
-        for quad in range(4):
-            queue = (nc.sync, nc.scalar)[quad % 2]
-            queue.dma_start(out=out_scales[4 * quad : 4 * quad + 4, :],
-                            in_=y_scales[32 * quad : 32 * quad + 4, :].bitcast(I32))
+        interleave_w(("w3", 0), 0, C, on_scalar, long_run)
+        interleave_p3(0, on_scalar, long_run)
+        quantize_p(2, 0)
+        quantize_x(2, 0, 2)
+        quantize_weight(("w1", 0))
+        interleave_w(("w2", 0), C // 2, C, on_vector, long_run)
+        quantize_x(3, 0, 2)
+        finish_p2(3)
+        for key in (("w1", 1), ("w3", 0), ("w2", 0)):
+            quantize_weight(key)
+        quantize_p(3, 0)
+        quantize_p(2, 1)
+
+        for q in range(2, QUARTERS):
+            for half in range(2):
+                project3(q, half)
+            project2(q + 2)
+        begin_p3(1, 1)
+        finish_p3(1, 1)
+        interleave_p3(1, on_gpsimd, short_run)
+        for q in range(2, QUARTERS):
+            for half in range(2):
+                begin_p3(q, half)
+                finish_p3(q, half)
+        quantize_p(3, 1)
+        sum_terms(0)
+        project2(6)
+        project2(7)
+        sum_terms(1)
+        for q in range(2, QUARTERS):
+            for i in (2 * q, 2 * q + 1):
+                begin_p2(i, True)
+            interleave_p3(q, on_scalar, long_run)
+        for q in range(2, QUARTERS):
+            for i in (2 * q, 2 * q + 1):
+                finish_p2(i)
+            store_y(q - 2)
+            quantize_p(3, q)
+            quantize_p(2, q)
+
+        for i in range(2):
+            round_y(i, on_scalar)
+        for i in range(2, TILES):
+            sum_terms(i)
+            store_y(i)
+            if i < TILES - 2:
+                round_y(i, on_scalar)
+        for i in range(TILES - 2, TILES):
+            round_y(i, on_vector)
+
+        for q in range(QUARTERS - 1):
+            transpose_y(2 * q, 2 * q + 2)
+            stage_y(2 * q, 2 * q + 2, on_scalar)
+        for i in range(TILES - 2, TILES):
+            transpose_y(i, i + 1)
+        store_planes(0)
+        stage_y(TILES - 2, TILES - 1, on_vector)
+        stage_y(TILES - 1, TILES, on_scalar)
+        for q in range(1, QUARTERS):
+            store_planes(q)
+        for quadrant in range(4):
+            queue = (nc.sync, nc.scalar)[quadrant % 2]
+            queue.dma_start(
+                out=out_scales[span(quadrant, 4), :],
+                in_=y_scales[32 * quadrant : 32 * quadrant + 4, :].bitcast(I32),
+            )

from contextlib import ExitStack

import concourse.mybir as mybir
from concourse.masks import make_identity

N, D, R, C = 1024, 1024, 512, 512
FLOPS = 2 * N * D * (2 * R + C) + 2 * 2 * N * R * C

F32 = mybir.dt.float32
BF16 = mybir.dt.bfloat16
U32 = mybir.dt.uint32
I32 = mybir.dt.int32
U8 = mybir.dt.uint8
FP8X4 = mybir.dt.float8_e4m3fn_x4
MULT = mybir.AluOpType.mult
ADD = mybir.AluOpType.add
SQUARE = mybir.ActivationFunctionType.Square

P = 128
SLOTS = 4
K_PASS = P * SLOTS
QUARTER = 2 * P
TILES, QUARTERS = N // P, N // QUARTER
BANKS, BANK_WORDS = 8, 512
ALIGN = 256
FIRST_FACTOR_BUFS = 8


def span(index, width):
    return slice(index * width, (index + 1) * width)


def tile_spamlowrankpolynomialorders_x1_kernel(tc, x, w1, u, lam, w, b, out_0, out_1, out_2):
    nc = tc.nc
    with ExitStack() as ctx:
        keep = ctx.enter_context(tc.tile_pool(name="keep", bufs=1))
        factors = ctx.enter_context(tc.tile_pool(name="factors", bufs=FIRST_FACTOR_BUFS))
        psum = ctx.enter_context(tc.psum_pool(name="psum", bufs=1))
        ctx.enter_context(tc.manual_schedule())

        def kept(name, shape, dtype):
            return keep.tile(shape, dtype, name=name, tag=name, align_bytes=ALIGN)

        weights = {}
        for g in range(D // K_PASS):
            weights["u2", g] = u[0, span(g, K_PASS), :]
            weights["u3", g] = u[1, span(g, K_PASS), :]
            weights["w1", g] = w1[span(g, K_PASS), :]
        weights["w2", 0] = w[0]
        weights["w3", 0] = w[1]
        rows = {key: kept("rows_%s_%d" % key, [P, SLOTS, 512], BF16) for key in weights}
        codes = {key: kept("codes_%s_%d" % key, [P, 512], U32) for key in weights}
        scales = {key: kept("scales_%s_%d" % key, [P, 512], U8) for key in weights}
        staged = {}

        x_rows = [kept("x_rows%d" % q, [P, 2, D], BF16) for q in range(QUARTERS)]
        x_staged = kept("x_staged", [P, QUARTERS, 2 * QUARTER * SLOTS], BF16)
        x_codes = kept("x_codes", [P, QUARTERS, 2 * QUARTER], U32)
        x_scales = kept("x_scales", [P, QUARTERS, 2 * QUARTER], U8)
        p3_rows = kept("p3_rows", [P, QUARTERS, SLOTS, QUARTER], BF16)
        p_staged = {order: kept("p%d_staged" % order, [P, N * SLOTS], BF16) for order in (2, 3)}
        p_codes = {order: kept("p%d_codes" % order, [P, N], U32) for order in (2, 3)}
        p_scales = {order: kept("p%d_scales" % order, [P, N], U8) for order in (2, 3)}
        y = [kept("y%d" % i, [P, C], F32) for i in range(TILES)]
        y_rounded = [kept("y_rounded%d" % i, [P, C], BF16) for i in range(TILES)]
        y_staged = kept("y_staged", [P, N * SLOTS], BF16)
        y_codes = kept("y_codes", [P, N], U32)
        y_scales = kept("y_scales", [P, N], U8)
        mask = kept("mask", [P, P], F32)
        identity = kept("identity", [P, P], F32)
        lam_sb = kept("lam_sb", [P, 2, SLOTS], BF16)
        bias = kept("bias", [P, C], BF16)
        lam2_by_token = lam_sb[:, 0, :].unsqueeze(1).to_broadcast([P, P, SLOTS])
        out_words = out_1[0].rearrange("p n j -> p (n j)").bitcast(I32)
        out_scales = out_2[0].bitcast(I32)
        banks = {}
        first_factor = {}
        second_factor = {}

        def new_bank(key):
            name = "bank%d" % (len(banks) % BANKS)
            banks[key] = psum.tile([P, BANK_WORDS], F32, name=name, tag=name)
            return banks[key]

        def on_vector(out, in_):
            nc.vector.tensor_copy(out=out, in_=in_)

        def on_scalar(out, in_):
            nc.scalar.copy(out=out, in_=in_)

        def on_gpsimd(out, in_):
            nc.gpsimd.tensor_scalar(out=out, in0=in_, scalar1=1.0, scalar2=0.0, op0=MULT, op1=ADD)

        def quantize(words, scale_bytes, in_):
            nc.vector.quantize_mx(out=words.bitcast(FP8X4), scales=scale_bytes, in_=in_)

        def multiply(out, passes):
            for index, (lhs_words, lhs_scales, rhs_words, rhs_scales) in enumerate(passes):
                nc.tensor.matmul_mx(
                    out=out,
                    lhsT=lhs_words.bitcast(FP8X4),
                    lhsT_scale=lhs_scales,
                    rhs=rhs_words.bitcast(FP8X4),
                    rhs_scale=rhs_scales,
                    start=index == 0,
                    stop=index == len(passes) - 1,
                )

        def interleave(copy, out, in_, run):
            copy(
                out.rearrange("p (c col j) -> p c j col", col=run, j=SLOTS),
                in_.rearrange("p j (c col) -> p c j col", col=run),
            )

        def load_weight(key):
            nc.sync.dma_start(out=rows[key][:], in_=weights[key].rearrange("(p j) c -> p j c", j=SLOTS))

        def staged_tile(key, tag):
            if key not in staged:
                staged[key] = kept("staged_%s_%d" % tag, [P, 512 * SLOTS], BF16)
            return staged[key]

        def interleave_u(key, half, copy):
            out = staged_tile(key, key)[:]
            out = out.rearrange("p (s line odd j) -> p line j odd s", s=SLOTS, odd=2, j=SLOTS)
            in_ = rows[key][:].rearrange("p j (line odd s) -> p line j odd s", odd=2, s=SLOTS)
            copy(out[:, :, :, :, span(half, 2)], in_[:, :, :, :, span(half, 2)])

        def interleave_w(key, first, last, copy, run, tag=None):
            out = staged_tile(key, tag or key)[:, SLOTS * first : SLOTS * last]
            interleave(copy, out, rows[key][:, :, first:last], run)

        def quantize_weight(key):
            quantize(codes[key][:], scales[key][:], staged[key][:])

        def load_x(q):
            nc.sync.dma_start(out=x_rows[q][:], in_=x[span(q, QUARTER), :].rearrange("(a n) d -> n a d", a=2))

        def transpose_x(q, g):
            bank = new_bank(("x", q, g))
            for a in range(2):
                words = x_rows[q][:, a, :].bitcast(F32)[:, span(g, K_PASS // 2)]
                for h in range(2):
                    nc.tensor.transpose(bank[:, span(2 * a + h, P)], words[:, h : K_PASS // 2 : 2], identity[:])

        def copy_words(copy, out, bank_part):
            copy(
                out.bitcast(F32).rearrange("p (a n h) -> p a n h", n=P, h=2),
                bank_part.rearrange("p (a h n) -> p a n h", h=2, n=P),
            )

        def stage_x(q, g, copy):
            copy_words(copy, x_staged[:, q, span(g, QUARTER * SLOTS)], banks["x", q, g][:])

        def quantize_x(q, first, last):
            columns = slice(QUARTER * first, QUARTER * last)
            in_ = x_staged[:, q, QUARTER * SLOTS * first : QUARTER * SLOTS * last]
            quantize(x_codes[:, q, columns], x_scales[:, q, columns], in_)

        def x_operand(g, first_token, tokens):
            q, offset = divmod(first_token, QUARTER)
            columns = slice(QUARTER * g + offset, QUARTER * g + offset + tokens)
            return x_codes[:, q, columns], x_scales[:, q, columns]

        def project(out, name, j, first_token, tokens):
            multiply(out, [
                (codes[name, g][:, span(j, P)], scales[name, g][:, span(j, P)]) + x_operand(g, first_token, tokens)
                for g in range(D // K_PASS)
            ])

        def project2(i):
            bank = new_bank(("q2", i))
            for j in range(SLOTS):
                project(bank[:, span(j, P)], "u2", j, P * i, P)

        def begin_p2(i, scalar_squares):
            factor = factors.tile([P, P, SLOTS], F32, name="factor", tag="factor")
            q2 = banks["q2", i][:].rearrange("p (j n) -> p n j", j=SLOTS)
            if scalar_squares:
                nc.scalar.activation(out=factor[:], in_=q2, func=SQUARE)
            else:
                nc.vector.tensor_tensor(out=factor[:], in0=q2, in1=lam2_by_token, op=MULT)
            first_factor[2, i] = factor
            second_factor[i] = lam2_by_token if scalar_squares else q2

        def finish_p2(i):
            out = p_staged[2][:, span(i, P * SLOTS)].rearrange("p (n j) -> p n j", j=SLOTS)
            nc.vector.tensor_tensor(out=out, in0=first_factor[2, i][:], in1=second_factor[i], op=MULT)

        def project3(q, half):
            bank = new_bank(("q3", q, half))
            for j in (2 * half, 2 * half + 1):
                project(bank[:, span(j % 2, QUARTER)], "u3", j, QUARTER * q, QUARTER)

        def begin_p3(q, half):
            factor = factors.tile([P, BANK_WORDS], F32, name="factor", tag="factor")
            nc.scalar.activation(out=factor[:], in_=banks["q3", q, half][:], func=SQUARE)
            first_factor[3, q, half] = factor

        def finish_p3(q, half):
            for j in (2 * half, 2 * half + 1):
                nc.vector.scalar_tensor_tensor(
                    out=p3_rows[:, q, j, :],
                    in0=first_factor[3, q, half][:, span(j % 2, QUARTER)],
                    scalar=lam_sb[:, 1, j : j + 1],
                    in1=banks["q3", q, half][:, span(j % 2, QUARTER)],
                    op0=MULT,
                    op1=MULT,
                )

        def interleave_p3(q, copy, run):
            interleave(copy, p_staged[3][:, span(q, QUARTER * SLOTS)], p3_rows[:, q, :, :], run)

        def quantize_p(order, q):
            columns = span(q, QUARTER)
            in_ = p_staged[order][:, span(q, QUARTER * SLOTS)]
            quantize(p_codes[order][:, columns], p_scales[order][:, columns], in_)

        def sum_terms(i):
            linear = [x_operand(g, P * i, P) + (codes["w1", g][:], scales["w1", g][:]) for g in range(D // K_PASS)]
            powers = [
                (p_codes[order][:, span(i, P)], p_scales[order][:, span(i, P)], codes[name, 0][:], scales[name, 0][:])
                for order, name in ((2, "w2"), (3, "w3"))
            ]
            multiply(new_bank(("y", i))[:], linear + powers)

        def store_y(i):
            nc.vector.tensor_tensor(out=y[i][:], in0=banks["y", i][:], in1=bias[:], op=ADD)
            nc.sync.dma_start(out=out_0[span(i, P), :], in_=y[i][:])

        def round_y(i, copy):
            copy(
                y_rounded[i][:].rearrange("p (h m e) -> p h m e", h=2, e=2),
                y[i][:].rearrange("p (m h e) -> p h m e", h=2, e=2),
            )

        def transpose_y(first, last):
            bank = new_bank(("yt", first))
            for i in range(first, last):
                words = y_rounded[i][:].bitcast(F32)
                for h in range(2):
                    nc.tensor.transpose(bank[:, span(2 * (i - first) + h, P)], words[:, span(h, P)], identity[:])

        def stage_y(first, last, copy):
            out = y_staged[:, P * SLOTS * first : P * SLOTS * last]
            copy_words(copy, out, banks["yt", first][:, : 2 * P * (last - first)])

        def store_planes(q):
            columns = span(q, QUARTER)
            quantize(y_codes[:, columns], y_scales[:, columns], y_staged[:, span(q, QUARTER * SLOTS)])
            nc.sync.dma_start(out=out_words[:, columns], in_=y_codes[:, columns].bitcast(I32))

        long_run, short_run = 4, 1

        make_identity(nc, mask[:])
        nc.scalar.activation(out=identity[:], in_=mask[:], func=SQUARE)
        nc.gpsimd.dma_start(out=lam_sb[:], in_=lam.rearrange("o (p j) -> p o j", j=SLOTS))

        for q, keys in enumerate(([("u2", 0), ("u2", 1)], [("u3", 0), ("u3", 1), ("w1", 0), ("w1", 1)],
                                  [("w2", 0)], [("w3", 0)])):
            load_x(q)
            for key in keys:
                load_weight(key)
        nc.sync.dma_start(out=bias[:], in_=b.partition_broadcast(P))

        for q in range(2):
            for g in range(2):
                transpose_x(q, g)
        interleave_u(("u2", 0), 0, on_scalar)
        interleave_u(("u2", 0), 1, on_vector)
        stage_x(0, 0, on_vector)
        interleave_u(("u2", 1), 0, on_vector)
        interleave_u(("u2", 1), 1, on_scalar)
        stage_x(0, 1, on_scalar)
        quantize_x(0, 0, 1)
        quantize_weight(("u2", 0))
        quantize_weight(("u2", 1))
        quantize_x(0, 1, 2)
        for g in range(2):
            stage_x(1, g, on_scalar)
        for half in range(2):
            interleave_u(("u3", 0), half, on_vector)
        interleave_u(("u3", 1), 0, on_scalar)
        interleave_u(("u3", 1), 1, on_vector)
        quantize_x(1, 0, 2)
        quantize_weight(("u3", 0))
        quantize_weight(("u3", 1))

        early_p3 = [(0, 0), (0, 1), (1, 0)]
        for i in range(4):
            project2(i)
        for q, half in early_p3:
            project3(q, half)
        interleave_w(("w1", 0), 0, C, on_scalar, long_run)
        interleave_w(("w1", 1), 0, C, on_gpsimd, short_run, tag=("u3", 1))
        interleave_w(("w2", 0), 0, C // 2, on_gpsimd, short_run)
        begin_p2(0, False)
        for i in range(1, 3):
            begin_p2(i, False)
            finish_p2(i - 1)
        finish_p2(2)
        begin_p3(0, 0)
        begin_p2(3, True)
        for q, half in early_p3[1:]:
            begin_p3(q, half)
        for q, half in early_p3:
            finish_p3(q, half)
        for q in range(2, QUARTERS):
            for g in range(2):
                transpose_x(q, g)
        for q in range(2, QUARTERS):
            for g in range(2):
                stage_x(q, g, on_scalar)
        project3(1, 1)

        interleave_w(("w3", 0), 0, C, on_scalar, long_run)
        interleave_p3(0, on_scalar, long_run)
        quantize_p(2, 0)
        quantize_x(2, 0, 2)
        quantize_weight(("w1", 0))
        interleave_w(("w2", 0), C // 2, C, on_vector, long_run)
        quantize_x(3, 0, 2)
        finish_p2(3)
        for key in (("w1", 1), ("w3", 0), ("w2", 0)):
            quantize_weight(key)
        quantize_p(3, 0)
        quantize_p(2, 1)

        for q in range(2, QUARTERS):
            for half in range(2):
                project3(q, half)
            project2(q + 2)
        begin_p3(1, 1)
        finish_p3(1, 1)
        interleave_p3(1, on_gpsimd, short_run)
        for q in range(2, QUARTERS):
            for half in range(2):
                begin_p3(q, half)
                finish_p3(q, half)
        quantize_p(3, 1)
        sum_terms(0)
        project2(6)
        project2(7)
        sum_terms(1)
        for q in range(2, QUARTERS):
            for i in (2 * q, 2 * q + 1):
                begin_p2(i, True)
            interleave_p3(q, on_scalar, long_run)
        for q in range(2, QUARTERS):
            for i in (2 * q, 2 * q + 1):
                finish_p2(i)
            store_y(q - 2)
            quantize_p(3, q)
            quantize_p(2, q)

        for i in range(2):
            round_y(i, on_scalar)
        for i in range(2, TILES):
            sum_terms(i)
            store_y(i)
            if i < TILES - 2:
                round_y(i, on_scalar)
        for i in range(TILES - 2, TILES):
            round_y(i, on_vector)

        for q in range(QUARTERS - 1):
            transpose_y(2 * q, 2 * q + 2)
            stage_y(2 * q, 2 * q + 2, on_scalar)
        for i in range(TILES - 2, TILES):
            transpose_y(i, i + 1)
        store_planes(0)
        stage_y(TILES - 2, TILES - 1, on_vector)
        stage_y(TILES - 1, TILES, on_scalar)
        for q in range(1, QUARTERS):
            store_planes(q)
        for quadrant in range(4):
            queue = (nc.sync, nc.scalar)[quadrant % 2]
            queue.dma_start(
                out=out_scales[span(quadrant, 4), :],
                in_=y_scales[32 * quadrant : 32 * quadrant + 4, :].bitcast(I32),
            )
